import numpy as np
import ml_dtypes


def mxq(x, axis, fmt="e4m3"):
    dtype, down = {"e4m3": (ml_dtypes.float8_e4m3fn, 7), "e5m2": (ml_dtypes.float8_e5m2, 14)}[fmt]
    v = np.moveaxis(np.asarray(x, np.float32).astype(ml_dtypes.bfloat16).astype(np.float64), axis, -1)
    blocks = v.reshape(v.shape[:-1] + (-1, 32))
    amax = np.abs(blocks).max(-1, keepdims=True)
    byte = np.maximum(np.where(amax > 0, np.frexp(amax)[1] - 1 + 127, 0) - down, 1)
    scale = np.exp2(byte - 127.0)
    codes = (blocks / scale).astype(np.float32).astype(dtype).astype(np.float64)
    return np.moveaxis((codes * scale).reshape(v.shape), -1, axis)


WIDE = False


def mx_kscale(k, group=512):
    if not WIDE:
        return np.ones(k)
    levels = np.array([18, -18])
    if group != 512:
        return np.exp2(np.random.permutation(np.resize(levels, k // group))).repeat(group)
    if k % 512:
        return np.exp2(np.random.permutation(np.resize(levels, k // 32))).repeat(32)
    a = np.empty((k // 512, 16))
    for p in range(k // 512):
        a[p, :8] = np.random.permutation(np.resize(levels, 8))
        for g in range(8):
            far = levels[np.abs(levels - a[p, g]) >= 10]
            a[p, g + 8] = far[np.random.randint(len(far))]
    return np.exp2(a.ravel()).repeat(32)


def f64(x):
    return np.asarray(x).astype(np.float64)


G, D, M, N = 4, 128, 128, 512


def setup_inputs():
    n = np.random.standard_normal
    s_d = mx_kscale(D, 0)
    return {
        "x": (n((G, D, N)) * s_d[:, None]).astype(np.float32),
        "w1": (n((G, D, M)) / np.sqrt(D) / s_d[:, None]).astype(np.float32),
        "w2": (n((G, D, M)) / np.sqrt(D) / s_d[:, None]).astype(np.float32),
        "sh": (np.random.uniform(0.1, 0.4, (G, M, 1))).astype(np.float32),
        "d0": (np.random.uniform(2.0, 6.0, (G, M, N))).astype(np.float32),
        "dx": (n((G, D, N)) * s_d[:, None]).astype(np.float32),
        "og": (np.random.uniform(0.5, 2.0, (G, M, 1))).astype(np.float32),
        "base": (0.3 * n((G, M, N))).astype(np.float32),
    }


def reference(x, w1, w2, sh, d0, dx, og, base):
    w1q = mxq(f64(w1), 1, "e4m3")
    xq = mxq(f64(x), 1, "e4m3")
    z1 = w1q.transpose(0, 2, 1) @ xq
    dxq = mxq(f64(dx), 1, "e4m3")
    tz1 = w1q.transpose(0, 2, 1) @ dxq
    w2q = mxq(f64(w2), 1, "e4m3")
    z2 = w2q.transpose(0, 2, 1) @ xq
    tz2 = w2q.transpose(0, 2, 1) @ dxq
    q1 = f64(d0) - z1 * 2.0
    xq1 = tz1 * 2.0 * (-1.0)
    xh = xq1 * f64(sh) * (-1.0) * np.exp(q1 * f64(sh) * (-1.0)) * z2 + tz2 * np.exp(q1 * f64(sh) * (-1.0))
    y = xh * f64(og) + f64(base)
    return y

@@ -1,0 +1,171 @@
+from contextlib import ExitStack
+
+import concourse.mybir as mybir
+
+G, D, M, N = 4, 128, 128, 512
+FLOPS = 4 * 2 * G * D * M * N
+
+F32 = mybir.dt.float32
+BF16 = mybir.dt.bfloat16
+U32 = mybir.dt.uint32
+U8 = mybir.dt.uint8
+FP8X4 = mybir.dt.float8_e4m3fn_x4
+ALU = mybir.AluOpType
+ACT = mybir.ActivationFunctionType
+
+P = 128
+PACK = 4
+ROWS = D // PACK
+HALF = N // 2
+SCALAR_COLS = 192
+
+
+def tile_rows_tnkernrbf_kernel(tc, x, w1, w2, sh, d0, dx, og, base, out):
+    nc = tc.nc
+
+    with ExitStack() as ctx:
+        sb = ctx.enter_context(tc.tile_pool(name="sb", bufs=1))
+        psum = ctx.enter_context(tc.psum_pool(name="psum", bufs=1))
+        ctx.enter_context(tc.manual_schedule())
+
+        def load_operand(name, src):
+            raw = sb.tile([P, PACK, src.shape[2]], F32, name=name + "_raw")
+            nc.sync.dma_start(out=raw[:], in_=src.rearrange("g (p j) c -> (g p) j c", j=PACK))
+            return raw
+
+        def load_rows(name, src, g):
+            rows = sb.tile([P, N], F32, name=name + str(g))
+            nc.sync.dma_start(out=rows[:], in_=src[g])
+            return rows
+
+        def load_column(name, src):
+            col = sb.tile([P, G, 8], F32, name=name)
+            with nc.allow_non_contiguous_dma(reason="one value a feature"):
+                nc.scalar.dma_start(out=col[:, :, 0:1], in_=src.rearrange("g m o -> m g o"))
+            return col
+
+        def interleave(copy, grouped, raw, c0, c1, at):
+            copy(
+                out=grouped[:, at : at + c1 - c0, :].rearrange("p (c i) j -> p c j i", i=4),
+                in_=raw[:, :, c0:c1].rearrange("p j (c i) -> p c j i", i=4),
+            )
+
+        def quantize(codes, scales, grouped, c0, c1):
+            nc.vector.quantize_mx(
+                out=codes[:, c0:c1].bitcast(FP8X4),
+                scales=scales[:, c0:c1],
+                in_=grouped[:].rearrange("p c j -> p (c j)"),
+            )
+
+        def mx_tiles(name, width):
+            codes = sb.tile([P, width], U32, name=name + "_codes", align_bytes=64)
+            scales = sb.tile([P, width], U8, name=name + "_scales", align_bytes=64)
+            return codes, scales
+
+        def product(bank, w, v, g):
+            rows = slice(ROWS * g, ROWS * (g + 1))
+            nc.tensor.matmul_mx(
+                out=bank[:],
+                lhsT=w[0][rows, :].bitcast(FP8X4),
+                lhsT_scale=w[1][rows, :],
+                rhs=v[0][rows, :].bitcast(FP8X4),
+                rhs_scale=v[1][rows, :],
+                start=True,
+                stop=True,
+            )
+
+        x_raw = load_operand("x", x)
+        sh_col = load_column("sh_col", sh)
+        og_col = load_column("og_col", og)
+        dx_raw = load_operand("dx", dx)
+        w1_raw = load_operand("w1", w1)
+        w2_raw = load_operand("w2", w2)
+        d0_sb = [load_rows("d0_", d0, g) for g in range(G)]
+        base_sb = [load_rows("base_", base, g) for g in range(G)]
+
+        def quantize_moving(name, raw):
+            q = mx_tiles(name, N)
+            lo = sb.tile([P, HALF, PACK], BF16, name=name + "_lo", align_bytes=64)
+            hi = sb.tile([P, HALF, PACK], BF16, name=name + "_hi", align_bytes=64)
+            cut = N - SCALAR_COLS
+            interleave(nc.scalar.copy, hi, raw, cut, N, cut - HALF)
+            interleave(nc.vector.tensor_copy, lo, raw, 0, HALF, 0)
+            interleave(nc.vector.tensor_copy, hi, raw, HALF, cut, 0)
+            quantize(q[0], q[1], lo, 0, HALF)
+            quantize(q[0], q[1], hi, HALF, N)
+            return q
+
+        def quantize_weights(name, raw):
+            q = mx_tiles(name, M)
+            grouped = sb.tile([P, M, PACK], BF16, name=name + "_bf", align_bytes=64)
+            interleave(nc.scalar.copy, grouped, raw, 0, M, 0)
+            quantize(q[0], q[1], grouped, 0, M)
+            return q
+
+        xq = quantize_moving("x", x_raw)
+        coef = sb.tile([P, G, 8], F32, name="coef")
+        nc.vector.scalar_tensor_tensor(
+            out=coef[:, :, 0], in0=sh_col[:, :, 0], scalar=2.0, in1=og_col[:, :, 0], op0=ALU.mult, op1=ALU.mult
+        )
+        dxq = quantize_moving("dx", dx_raw)
+        w1q = quantize_weights("w1", w1_raw)
+        w2q = quantize_weights("w2", w2_raw)
+
+        def bank(kind, g, name):
+            return psum.tile([P, N], F32, name=name + str(g), tag=kind + str(g))
+
+        def work(name):
+            return [sb.tile([P, N], F32, name=name + str(g)) for g in range(G)]
+
+        z1 = [bank("first", g, "z1_") for g in range(G)]
+        z2 = [bank("second", g, "z2_") for g in range(G)]
+        for g in range(G):
+            product(z1[g], w1q, xq, g)
+        for g in range(G):
+            product(z2[g], w2q, xq, g)
+
+        negq, gauss, z2s, cross, inner, xh, res = [
+            work(s) for s in ("negq", "gauss", "z2s", "cross", "inner", "xh", "res")
+        ]
+        tz1, tz2 = {}, {}
+
+        def front(g):
+            nc.vector.scalar_tensor_tensor(
+                out=negq[g][:], in0=z1[g][:], scalar=2.0, in1=d0_sb[g][:], op0=ALU.mult, op1=ALU.subtract
+            )
+            nc.scalar.activation(out=z2s[g][:], in_=z2[g][:], func=ACT.Copy, scale=coef[:, g, 0:1])
+            nc.scalar.activation(out=gauss[g][:], in_=negq[g][:], func=ACT.Exp, scale=sh_col[:, g, 0:1])
+            tz1[g] = bank("first", g, "tz1_")
+            product(tz1[g], w1q, dxq, g)
+            tz2[g] = bank("second", g, "tz2_")
+            product(tz2[g], w2q, dxq, g)
+
+        def middle(g):
+            halves = [slice(0, HALF), slice(HALF, N)]
+            for cols in halves:
+                nc.vector.tensor_tensor(out=cross[g][:, cols], in0=tz1[g][:, cols], in1=z2s[g][:, cols], op=ALU.mult)
+            for cols in halves:
+                nc.vector.scalar_tensor_tensor(
+                    out=inner[g][:, cols], in0=tz2[g][:, cols], scalar=og_col[:, g, 0:1], in1=cross[g][:, cols],
+                    op0=ALU.mult, op1=ALU.add,
+                )
+
+        def weigh(engine, g):
+            engine.tensor_tensor(out=xh[g][:], in0=inner[g][:], in1=gauss[g][:], op=ALU.mult)
+
+        def finish(engine, g):
+            engine.tensor_tensor(out=res[g][:], in0=xh[g][:], in1=base_sb[g][:], op=ALU.add)
+            nc.sync.dma_start(out=out[g], in_=res[g][:])
+
+        front(0)
+        for g in range(G):
+            if g + 1 < G:
+                front(g + 1)
+            middle(g)
+            if g < 2:
+                weigh(nc.gpsimd, g)
+                finish(nc.gpsimd, g)
+        for g in (2, 3):
+            weigh(nc.vector, g)
+        for g in (2, 3):
+            finish(nc.vector, g)

@@ -17,7 +17,8 @@ P = 128
 PACK = 4
 ROWS = D // PACK
 HALF = N // 2
-SCALAR_COLS = 192
+N_MM = 128
+VECTOR_COLS = 160
 
 
 def tile_rows_tnkernrbf_kernel(tc, x, w1, w2, sh, d0, dx, og, base, out):
@@ -28,144 +29,177 @@ def tile_rows_tnkernrbf_kernel(tc, x, w1, w2, sh, d0, dx, og, base, out):
         psum = ctx.enter_context(tc.psum_pool(name="psum", bufs=1))
         ctx.enter_context(tc.manual_schedule())
 
+        def half_cols(h):
+            return slice(h * HALF, (h + 1) * HALF)
+
         def load_operand(name, src):
             raw = sb.tile([P, PACK, src.shape[2]], F32, name=name + "_raw")
             nc.sync.dma_start(out=raw[:], in_=src.rearrange("g (p j) c -> (g p) j c", j=PACK))
             return raw
 
-        def load_rows(name, src, g):
-            rows = sb.tile([P, N], F32, name=name + str(g))
-            nc.sync.dma_start(out=rows[:], in_=src[g])
+        def load_rows(name, src):
+            rows = sb.tile([P, G, HALF], F32, name=name)
+            nc.sync.dma_start(out=rows[:], in_=src.rearrange("g m c -> m g c"))
             return rows
 
-        def load_column(name, src):
-            col = sb.tile([P, G, 8], F32, name=name)
-            with nc.allow_non_contiguous_dma(reason="one value a feature"):
-                nc.scalar.dma_start(out=col[:, :, 0:1], in_=src.rearrange("g m o -> m g o"))
-            return col
-
-        def interleave(copy, grouped, raw, c0, c1, at):
+        def interleave(copy, grouped, raw, c0, c1):
             copy(
-                out=grouped[:, at : at + c1 - c0, :].rearrange("p (c i) j -> p c j i", i=4),
+                out=grouped[:, c0:c1, :].rearrange("p (c i) j -> p c j i", i=4),
                 in_=raw[:, :, c0:c1].rearrange("p j (c i) -> p c j i", i=4),
             )
 
-        def quantize(codes, scales, grouped, c0, c1):
-            nc.vector.quantize_mx(
-                out=codes[:, c0:c1].bitcast(FP8X4),
-                scales=scales[:, c0:c1],
-                in_=grouped[:].rearrange("p c j -> p (c j)"),
-            )
+        def round_operand(name, raw, vector_cols):
+            width = raw.shape[2]
+            grouped = sb.tile([P, width, PACK], BF16, name=name + "_bf", align_bytes=64)
+            if vector_cols < width:
+                interleave(nc.scalar.copy, grouped, raw, vector_cols, width)
+            if vector_cols > 0:
+                interleave(nc.vector.tensor_copy, grouped, raw, 0, vector_cols)
+            return grouped
 
-        def mx_tiles(name, width):
+        def quantize(name, grouped):
+            width = grouped.shape[1]
             codes = sb.tile([P, width], U32, name=name + "_codes", align_bytes=64)
             scales = sb.tile([P, width], U8, name=name + "_scales", align_bytes=64)
+            nc.vector.quantize_mx(
+                out=codes[:].bitcast(FP8X4), scales=scales[:], in_=grouped[:].rearrange("p c j -> p (c j)")
+            )
             return codes, scales
 
-        def product(bank, w, v, g):
-            rows = slice(ROWS * g, ROWS * (g + 1))
-            nc.tensor.matmul_mx(
-                out=bank[:],
-                lhsT=w[0][rows, :].bitcast(FP8X4),
-                lhsT_scale=w[1][rows, :],
-                rhs=v[0][rows, :].bitcast(FP8X4),
-                rhs_scale=v[1][rows, :],
-                start=True,
-                stop=True,
-            )
+        def product(banks, which, w, v, pair):
+            for c0 in range(0, HALF, N_MM):
+                cols = slice(c0, c0 + N_MM)
+                for g in pair:
+                    rows = slice(ROWS * g, ROWS * (g + 1))
+                    nc.tensor.matmul_mx(
+                        out=banks[g][:, which, cols],
+                        lhsT=w[0][rows, :].bitcast(FP8X4),
+                        lhsT_scale=w[1][rows, :],
+                        rhs=v[0][rows, cols].bitcast(FP8X4),
+                        rhs_scale=v[1][rows, cols],
+                        start=True,
+                        stop=True,
+                    )
 
-        x_raw = load_operand("x", x)
-        sh_col = load_column("sh_col", sh)
-        og_col = load_column("og_col", og)
-        dx_raw = load_operand("dx", dx)
         w1_raw = load_operand("w1", w1)
+        feat_rows = sb.tile([P, 32], F32, name="feat_rows", align_bytes=64)
+        nc.gpsimd.memset(feat_rows[:], 0.0)
+        for k, src in enumerate((sh, og)):
+            nc.sync.dma_start(out=feat_rows[k:P:8, :], in_=src.rearrange("g (b i) o -> b g (i o)", i=32))
+        feat = sb.tile([P, G, 8], F32, name="feat", align_bytes=64)
         w2_raw = load_operand("w2", w2)
-        d0_sb = [load_rows("d0_", d0, g) for g in range(G)]
-        base_sb = [load_rows("base_", base, g) for g in range(G)]
-
-        def quantize_moving(name, raw):
-            q = mx_tiles(name, N)
-            lo = sb.tile([P, HALF, PACK], BF16, name=name + "_lo", align_bytes=64)
-            hi = sb.tile([P, HALF, PACK], BF16, name=name + "_hi", align_bytes=64)
-            cut = N - SCALAR_COLS
-            interleave(nc.scalar.copy, hi, raw, cut, N, cut - HALF)
-            interleave(nc.vector.tensor_copy, lo, raw, 0, HALF, 0)
-            interleave(nc.vector.tensor_copy, hi, raw, HALF, cut, 0)
-            quantize(q[0], q[1], lo, 0, HALF)
-            quantize(q[0], q[1], hi, HALF, N)
-            return q
-
-        def quantize_weights(name, raw):
-            q = mx_tiles(name, M)
-            grouped = sb.tile([P, M, PACK], BF16, name=name + "_bf", align_bytes=64)
-            interleave(nc.scalar.copy, grouped, raw, 0, M, 0)
-            quantize(q[0], q[1], grouped, 0, M)
-            return q
-
-        xq = quantize_moving("x", x_raw)
-        coef = sb.tile([P, G, 8], F32, name="coef")
-        nc.vector.scalar_tensor_tensor(
-            out=coef[:, :, 0], in0=sh_col[:, :, 0], scalar=2.0, in1=og_col[:, :, 0], op0=ALU.mult, op1=ALU.mult
-        )
-        dxq = quantize_moving("dx", dx_raw)
-        w1q = quantize_weights("w1", w1_raw)
-        w2q = quantize_weights("w2", w2_raw)
-
-        def bank(kind, g, name):
-            return psum.tile([P, N], F32, name=name + str(g), tag=kind + str(g))
+        x_raw, dx_raw, d0_sb = [], [], []
+        for h in range(2):
+            x_raw.append(load_operand("x%d" % h, x[:, :, half_cols(h)]))
+            dx_raw.append(load_operand("dx%d" % h, dx[:, :, half_cols(h)]))
+            d0_sb.append(load_rows("d0_%d" % h, d0[:, :, half_cols(h)]))
+        base_sb = [load_rows("base_%d" % h, base[:, :, half_cols(h)]) for h in range(2)]
 
         def work(name):
-            return [sb.tile([P, N], F32, name=name + str(g)) for g in range(G)]
-
-        z1 = [bank("first", g, "z1_") for g in range(G)]
-        z2 = [bank("second", g, "z2_") for g in range(G)]
-        for g in range(G):
-            product(z1[g], w1q, xq, g)
-        for g in range(G):
-            product(z2[g], w2q, xq, g)
+            return [sb.tile([P, G, HALF], F32, name=name + str(h)) for h in range(2)]
 
         negq, gauss, z2s, cross, inner, xh, res = [
             work(s) for s in ("negq", "gauss", "z2s", "cross", "inner", "xh", "res")
         ]
-        tz1, tz2 = {}, {}
+        coef = sb.tile([P, G, 8], F32, name="coef")
+        z_bank = [psum.tile([P, 2, HALF], F32, name="z_bank%d" % g) for g in range(G)]
+        tz_bank = [psum.tile([P, 2, HALF], F32, name="tz_bank%d" % g) for g in range(G)]
 
-        def front(g):
+        def distance(h, g):
             nc.vector.scalar_tensor_tensor(
-                out=negq[g][:], in0=z1[g][:], scalar=2.0, in1=d0_sb[g][:], op0=ALU.mult, op1=ALU.subtract
+                out=negq[h][:, g, :], in0=z_bank[g][:, 0, :], scalar=2.0, in1=d0_sb[h][:, g, :],
+                op0=ALU.mult, op1=ALU.subtract,
             )
-            nc.scalar.activation(out=z2s[g][:], in_=z2[g][:], func=ACT.Copy, scale=coef[:, g, 0:1])
-            nc.scalar.activation(out=gauss[g][:], in_=negq[g][:], func=ACT.Exp, scale=sh_col[:, g, 0:1])
-            tz1[g] = bank("first", g, "tz1_")
-            product(tz1[g], w1q, dxq, g)
-            tz2[g] = bank("second", g, "tz2_")
-            product(tz2[g], w2q, dxq, g)
 
-        def middle(g):
-            halves = [slice(0, HALF), slice(HALF, N)]
-            for cols in halves:
-                nc.vector.tensor_tensor(out=cross[g][:, cols], in0=tz1[g][:, cols], in1=z2s[g][:, cols], op=ALU.mult)
-            for cols in halves:
-                nc.vector.scalar_tensor_tensor(
-                    out=inner[g][:, cols], in0=tz2[g][:, cols], scalar=og_col[:, g, 0:1], in1=cross[g][:, cols],
-                    op0=ALU.mult, op1=ALU.add,
-                )
+        def exponential(h, g):
+            nc.scalar.activation(out=gauss[h][:, g, :], in_=negq[h][:, g, :], func=ACT.Exp, scale=feat[:, g, 0:1])
 
-        def weigh(engine, g):
-            engine.tensor_tensor(out=xh[g][:], in0=inner[g][:], in1=gauss[g][:], op=ALU.mult)
+        def scale_z2(h, g):
+            nc.scalar.activation(out=z2s[h][:, g, :], in_=z_bank[g][:, 1, :], func=ACT.Copy, scale=coef[:, g, 0:1])
 
-        def finish(engine, g):
-            engine.tensor_tensor(out=res[g][:], in0=xh[g][:], in1=base_sb[g][:], op=ALU.add)
-            nc.sync.dma_start(out=out[g], in_=res[g][:])
+        def cross_term(h, g):
+            nc.vector.tensor_tensor(out=cross[h][:, g, :], in0=tz_bank[g][:, 0, :], in1=z2s[h][:, g, :], op=ALU.mult)
 
-        front(0)
-        for g in range(G):
-            if g + 1 < G:
-                front(g + 1)
-            middle(g)
-            if g < 2:
-                weigh(nc.gpsimd, g)
-                finish(nc.gpsimd, g)
-        for g in (2, 3):
-            weigh(nc.vector, g)
-        for g in (2, 3):
-            finish(nc.vector, g)
+        def inner_sum(h, g):
+            nc.vector.scalar_tensor_tensor(
+                out=inner[h][:, g, :], in0=tz_bank[g][:, 1, :], scalar=feat[:, g, 1:2], in1=cross[h][:, g, :],
+                op0=ALU.mult, op1=ALU.add,
+            )
+
+        def weigh(engine, h, gs):
+            engine.tensor_tensor(out=xh[h][:, gs, :], in0=inner[h][:, gs, :], in1=gauss[h][:, gs, :], op=ALU.mult)
+
+        def finish(engine, h, gs):
+            engine.tensor_tensor(out=res[h][:, gs, :], in0=xh[h][:, gs, :], in1=base_sb[h][:, gs, :], op=ALU.add)
+            nc.sync.dma_start(out=out[gs, :, half_cols(h)].rearrange("g m c -> m g c"), in_=res[h][:, gs, :])
+
+        def z_products(h, pair):
+            product(z_bank, 1, w2q, xq[h], pair)
+            product(z_bank, 0, w1q, xq[h], pair)
+
+        def tz_products(h, pair):
+            product(tz_bank, 0, w1q, dxq[h], pair)
+            product(tz_bank, 1, w2q, dxq[h], pair)
+
+        def z_readers(h, pair):
+            for g in pair:
+                scale_z2(h, g)
+            for g in pair:
+                distance(h, g)
+            for g in pair:
+                exponential(h, g)
+
+        def tz_readers(h, pair):
+            for g in pair:
+                cross_term(h, g)
+            for g in pair:
+                inner_sum(h, g)
+
+        def gpsimd_round(out, in_):
+            nc.gpsimd.tensor_scalar(out=out, in0=in_, scalar1=1.0, scalar2=0.0, op0=ALU.mult, op1=ALU.add)
+
+        low, high = (0, 1), (2, 3)
+        xq, dxq = {}, {}
+
+        w1_bf = round_operand("w1", w1_raw, M)
+        w2_bf = round_operand("w2", w2_raw, M)
+        w1q = quantize("w1", w1_bf)
+        nc.vector.transpose(feat[:].rearrange("p g k -> p (g k)"), feat_rows[:])
+        w2q = quantize("w2", w2_bf)
+        nc.vector.scalar_tensor_tensor(
+            out=coef[:, :, 0], in0=feat[:, :, 0], scalar=2.0, in1=feat[:, :, 1], op0=ALU.mult, op1=ALU.mult
+        )
+        xq[0] = quantize("x0", round_operand("x0", x_raw[0], VECTOR_COLS))
+        dxq[0] = quantize("dx0", round_operand("dx0", dx_raw[0], VECTOR_COLS))
+        x1_bf = sb.tile([P, HALF, PACK], BF16, name="x1_bf", align_bytes=64)
+        interleave(gpsimd_round, x1_bf, x_raw[1], 0, HALF)
+
+        z_products(0, low)
+        tz_products(0, low)
+        z_products(0, high)
+        tz_products(0, high)
+        z_readers(0, low)
+        tz_readers(0, low)
+        z_readers(0, high)
+        weigh(nc.gpsimd, 0, slice(0, 2))
+        finish(nc.gpsimd, 0, slice(0, 2))
+        xq[1] = quantize("x1", x1_bf)
+        dx1_bf = round_operand("dx1", dx_raw[1], 0)
+        tz_readers(0, high)
+        weigh(nc.gpsimd, 0, slice(2, 4))
+        finish(nc.gpsimd, 0, slice(2, 4))
+        dxq[1] = quantize("dx1", dx1_bf)
+
+        z_products(1, low)
+        tz_products(1, low)
+        z_products(1, high)
+        tz_products(1, high)
+        z_readers(1, low)
+        tz_readers(1, low)
+        z_readers(1, high)
+        tz_readers(1, high)
+        weigh(nc.vector, 1, slice(0, 2))
+        weigh(nc.vector, 1, slice(2, 4))
+        finish(nc.vector, 1, slice(0, 2))
+        finish(nc.vector, 1, slice(2, 3))
+        finish(nc.vector, 1, slice(3, 4))

@@ -16,9 +16,10 @@ ACT = mybir.ActivationFunctionType
 P = 128
 PACK = 4
 ROWS = D // PACK
-HALF = N // 2
 N_MM = 128
-VECTOR_COLS = 160
+EDGES = (0, 256, 512)
+PIECES = len(EDGES) - 1
+VECTOR_SHARE = 80
 
 
 def tile_rows_tnkernrbf_kernel(tc, x, w1, w2, sh, d0, dx, og, base, out):
@@ -29,8 +30,11 @@ def tile_rows_tnkernrbf_kernel(tc, x, w1, w2, sh, d0, dx, og, base, out):
         psum = ctx.enter_context(tc.psum_pool(name="psum", bufs=1))
         ctx.enter_context(tc.manual_schedule())
 
-        def half_cols(h):
-            return slice(h * HALF, (h + 1) * HALF)
+        def cols(k):
+            return slice(EDGES[k], EDGES[k + 1])
+
+        def width(k):
+            return EDGES[k + 1] - EDGES[k]
 
         def load_operand(name, src):
             raw = sb.tile([P, PACK, src.shape[2]], F32, name=name + "_raw")
@@ -38,7 +42,7 @@ def tile_rows_tnkernrbf_kernel(tc, x, w1, w2, sh, d0, dx, og, base, out):
             return raw
 
         def load_rows(name, src):
-            rows = sb.tile([P, G, HALF], F32, name=name)
+            rows = sb.tile([P, G, src.shape[2]], F32, name=name)
             nc.sync.dma_start(out=rows[:], in_=src.rearrange("g m c -> m g c"))
             return rows
 
@@ -49,157 +53,200 @@ def tile_rows_tnkernrbf_kernel(tc, x, w1, w2, sh, d0, dx, og, base, out):
             )
 
         def round_operand(name, raw, vector_cols):
-            width = raw.shape[2]
-            grouped = sb.tile([P, width, PACK], BF16, name=name + "_bf", align_bytes=64)
-            if vector_cols < width:
-                interleave(nc.scalar.copy, grouped, raw, vector_cols, width)
+            n_cols = raw.shape[2]
+            grouped = sb.tile([P, n_cols, PACK], BF16, name=name + "_bf", align_bytes=64)
+            if vector_cols < n_cols:
+                interleave(nc.scalar.copy, grouped, raw, vector_cols, n_cols)
             if vector_cols > 0:
                 interleave(nc.vector.tensor_copy, grouped, raw, 0, vector_cols)
             return grouped
 
         def quantize(name, grouped):
-            width = grouped.shape[1]
-            codes = sb.tile([P, width], U32, name=name + "_codes", align_bytes=64)
-            scales = sb.tile([P, width], U8, name=name + "_scales", align_bytes=64)
+            n_cols = grouped.shape[1]
+            codes = sb.tile([P, n_cols], U32, name=name + "_codes", align_bytes=64)
+            scales = sb.tile([P, n_cols], U8, name=name + "_scales", align_bytes=64)
             nc.vector.quantize_mx(
                 out=codes[:].bitcast(FP8X4), scales=scales[:], in_=grouped[:].rearrange("p c j -> p (c j)")
             )
             return codes, scales
 
-        def product(banks, which, w, v, pair):
-            for c0 in range(0, HALF, N_MM):
-                cols = slice(c0, c0 + N_MM)
-                for g in pair:
+        def product(banks, which, w, v, groups=range(G)):
+            for c0 in range(0, v[0].shape[1], N_MM):
+                span = slice(c0, c0 + N_MM)
+                for g in groups:
                     rows = slice(ROWS * g, ROWS * (g + 1))
                     nc.tensor.matmul_mx(
-                        out=banks[g][:, which, cols],
+                        out=banks[g][:, which, span],
                         lhsT=w[0][rows, :].bitcast(FP8X4),
                         lhsT_scale=w[1][rows, :],
-                        rhs=v[0][rows, cols].bitcast(FP8X4),
-                        rhs_scale=v[1][rows, cols],
+                        rhs=v[0][rows, span].bitcast(FP8X4),
+                        rhs_scale=v[1][rows, span],
                         start=True,
                         stop=True,
                     )
 
-        w1_raw = load_operand("w1", w1)
+        x_raw, dx_raw, d0_sb, base_sb = {}, {}, {}, {}
+
+        def load_x(k):
+            x_raw[k] = load_operand("x%d" % k, x[:, :, cols(k)])
+
+        def load_dx(k):
+            dx_raw[k] = load_operand("dx%d" % k, dx[:, :, cols(k)])
+
+        def load_d0(k0, k1):
+            rows = load_rows("d0_%d" % k0, d0[:, :, EDGES[k0] : EDGES[k1]])
+            for k in range(k0, k1):
+                d0_sb[k] = rows[:, :, EDGES[k] - EDGES[k0] : EDGES[k + 1] - EDGES[k0]]
+
+        def load_base(k0, k1):
+            rows = load_rows("base_%d" % k0, base[:, :, EDGES[k0] : EDGES[k1]])
+            for k in range(k0, k1):
+                base_sb[k] = rows[:, :, EDGES[k] - EDGES[k0] : EDGES[k + 1] - EDGES[k0]]
+
+        w2_raw = load_operand("w2", w2)
         feat_rows = sb.tile([P, 32], F32, name="feat_rows", align_bytes=64)
         nc.gpsimd.memset(feat_rows[:], 0.0)
+        load_x(0)
         for k, src in enumerate((sh, og)):
             nc.sync.dma_start(out=feat_rows[k:P:8, :], in_=src.rearrange("g (b i) o -> b g (i o)", i=32))
-        feat = sb.tile([P, G, 8], F32, name="feat", align_bytes=64)
-        w2_raw = load_operand("w2", w2)
-        x_raw, dx_raw, d0_sb = [], [], []
-        for h in range(2):
-            x_raw.append(load_operand("x%d" % h, x[:, :, half_cols(h)]))
-            dx_raw.append(load_operand("dx%d" % h, dx[:, :, half_cols(h)]))
-            d0_sb.append(load_rows("d0_%d" % h, d0[:, :, half_cols(h)]))
-        base_sb = [load_rows("base_%d" % h, base[:, :, half_cols(h)]) for h in range(2)]
+        w1_raw = load_operand("w1", w1)
+        load_dx(0)
+        load_d0(0, 1)
+        load_x(1)
+        load_dx(1)
+        load_d0(1, 2)
+        load_base(0, 1)
+        load_base(1, 2)
 
         def work(name):
-            return [sb.tile([P, G, HALF], F32, name=name + str(h)) for h in range(2)]
+            return [sb.tile([P, G, width(k)], F32, name=name + str(k)) for k in range(PIECES)]
 
         negq, gauss, z2s, cross, inner, xh, res = [
             work(s) for s in ("negq", "gauss", "z2s", "cross", "inner", "xh", "res")
         ]
+        feat = sb.tile([P, G, 8], F32, name="feat", align_bytes=64)
         coef = sb.tile([P, G, 8], F32, name="coef")
-        z_bank = [psum.tile([P, 2, HALF], F32, name="z_bank%d" % g) for g in range(G)]
-        tz_bank = [psum.tile([P, 2, HALF], F32, name="tz_bank%d" % g) for g in range(G)]
+        w1_bank = [psum.tile([P, 2, 256], F32, name="w1_bank%d" % g) for g in range(G)]
+        w2_bank = [psum.tile([P, 2, 256], F32, name="w2_bank%d" % g) for g in range(G)]
+        xq, dxq, x_bf, dx_bf = {}, {}, {}, {}
 
-        def distance(h, g):
-            nc.vector.scalar_tensor_tensor(
-                out=negq[h][:, g, :], in0=z_bank[g][:, 0, :], scalar=2.0, in1=d0_sb[h][:, g, :],
-                op0=ALU.mult, op1=ALU.subtract,
-            )
+        def distance(k, groups):
+            for g in groups:
+                nc.vector.scalar_tensor_tensor(
+                    out=negq[k][:, g, :], in0=w1_bank[g][:, 0, : width(k)], scalar=2.0, in1=d0_sb[k][:, g, :],
+                    op0=ALU.mult, op1=ALU.subtract,
+                )
 
-        def exponential(h, g):
-            nc.scalar.activation(out=gauss[h][:, g, :], in_=negq[h][:, g, :], func=ACT.Exp, scale=feat[:, g, 0:1])
+        def exponential(k, groups):
+            for g in groups:
+                nc.scalar.activation(out=gauss[k][:, g, :], in_=negq[k][:, g, :], func=ACT.Exp, scale=feat[:, g, 0:1])
 
-        def scale_z2(h, g):
-            nc.scalar.activation(out=z2s[h][:, g, :], in_=z_bank[g][:, 1, :], func=ACT.Copy, scale=coef[:, g, 0:1])
+        def scale_z2(k, groups):
+            for g in groups:
+                nc.scalar.activation(
+                    out=z2s[k][:, g, :], in_=w2_bank[g][:, 0, : width(k)], func=ACT.Copy, scale=coef[:, g, 0:1]
+                )
 
-        def cross_term(h, g):
-            nc.vector.tensor_tensor(out=cross[h][:, g, :], in0=tz_bank[g][:, 0, :], in1=z2s[h][:, g, :], op=ALU.mult)
+        def cross_term(k, groups):
+            for g in groups:
+                nc.vector.tensor_tensor(
+                    out=cross[k][:, g, :], in0=w1_bank[g][:, 1, : width(k)], in1=z2s[k][:, g, :], op=ALU.mult
+                )
 
-        def inner_sum(h, g):
-            nc.vector.scalar_tensor_tensor(
-                out=inner[h][:, g, :], in0=tz_bank[g][:, 1, :], scalar=feat[:, g, 1:2], in1=cross[h][:, g, :],
-                op0=ALU.mult, op1=ALU.add,
-            )
+        def inner_sum(k, groups):
+            for g in groups:
+                nc.vector.scalar_tensor_tensor(
+                    out=inner[k][:, g, :], in0=w2_bank[g][:, 1, : width(k)], scalar=feat[:, g, 1:2],
+                    in1=cross[k][:, g, :], op0=ALU.mult, op1=ALU.add,
+                )
 
-        def weigh(engine, h, gs):
-            engine.tensor_tensor(out=xh[h][:, gs, :], in0=inner[h][:, gs, :], in1=gauss[h][:, gs, :], op=ALU.mult)
+        def weigh(engine, k, gs=slice(0, G)):
+            engine.tensor_tensor(out=xh[k][:, gs, :], in0=inner[k][:, gs, :], in1=gauss[k][:, gs, :], op=ALU.mult)
 
-        def finish(engine, h, gs):
-            engine.tensor_tensor(out=res[h][:, gs, :], in0=xh[h][:, gs, :], in1=base_sb[h][:, gs, :], op=ALU.add)
-            nc.sync.dma_start(out=out[gs, :, half_cols(h)].rearrange("g m c -> m g c"), in_=res[h][:, gs, :])
+        def finish(engine, k, gs=slice(0, G)):
+            engine.tensor_tensor(out=res[k][:, gs, :], in0=xh[k][:, gs, :], in1=base_sb[k][:, gs, :], op=ALU.add)
+            nc.sync.dma_start(out=out[gs, :, cols(k)].rearrange("g m c -> m g c"), in_=res[k][:, gs, :])
 
-        def z_products(h, pair):
-            product(z_bank, 1, w2q, xq[h], pair)
-            product(z_bank, 0, w1q, xq[h], pair)
+        def round_x(k, vector_cols=0):
+            x_bf[k] = round_operand("x%d" % k, x_raw[k], vector_cols)
 
-        def tz_products(h, pair):
-            product(tz_bank, 0, w1q, dxq[h], pair)
-            product(tz_bank, 1, w2q, dxq[h], pair)
+        def round_dx(k, vector_cols=0):
+            dx_bf[k] = round_operand("dx%d" % k, dx_raw[k], vector_cols)
 
-        def z_readers(h, pair):
-            for g in pair:
-                scale_z2(h, g)
-            for g in pair:
-                distance(h, g)
-            for g in pair:
-                exponential(h, g)
+        def quantize_x(k):
+            xq[k] = quantize("x%d" % k, x_bf[k])
 
-        def tz_readers(h, pair):
-            for g in pair:
-                cross_term(h, g)
-            for g in pair:
-                inner_sum(h, g)
+        def quantize_dx(k):
+            dxq[k] = quantize("dx%d" % k, dx_bf[k])
 
-        def gpsimd_round(out, in_):
-            nc.gpsimd.tensor_scalar(out=out, in0=in_, scalar1=1.0, scalar2=0.0, op0=ALU.mult, op1=ALU.add)
-
-        low, high = (0, 1), (2, 3)
-        xq, dxq = {}, {}
-
-        w1_bf = round_operand("w1", w1_raw, M)
-        w2_bf = round_operand("w2", w2_raw, M)
-        w1q = quantize("w1", w1_bf)
+        w2q = quantize("w2", round_operand("w2", w2_raw, VECTOR_SHARE))
+        round_x(0, VECTOR_SHARE * width(0) // 128)
+        quantize_x(0)
         nc.vector.transpose(feat[:].rearrange("p g k -> p (g k)"), feat_rows[:])
-        w2q = quantize("w2", w2_bf)
+        w1_bf = round_operand("w1", w1_raw, VECTOR_SHARE)
         nc.vector.scalar_tensor_tensor(
             out=coef[:, :, 0], in0=feat[:, :, 0], scalar=2.0, in1=feat[:, :, 1], op0=ALU.mult, op1=ALU.mult
         )
-        xq[0] = quantize("x0", round_operand("x0", x_raw[0], VECTOR_COLS))
-        dxq[0] = quantize("dx0", round_operand("dx0", dx_raw[0], VECTOR_COLS))
-        x1_bf = sb.tile([P, HALF, PACK], BF16, name="x1_bf", align_bytes=64)
-        interleave(gpsimd_round, x1_bf, x_raw[1], 0, HALF)
-
-        z_products(0, low)
-        tz_products(0, low)
-        z_products(0, high)
-        tz_products(0, high)
-        z_readers(0, low)
-        tz_readers(0, low)
-        z_readers(0, high)
-        weigh(nc.gpsimd, 0, slice(0, 2))
-        finish(nc.gpsimd, 0, slice(0, 2))
-        xq[1] = quantize("x1", x1_bf)
-        dx1_bf = round_operand("dx1", dx_raw[1], 0)
-        tz_readers(0, high)
-        weigh(nc.gpsimd, 0, slice(2, 4))
-        finish(nc.gpsimd, 0, slice(2, 4))
-        dxq[1] = quantize("dx1", dx1_bf)
-
-        z_products(1, low)
-        tz_products(1, low)
-        z_products(1, high)
-        tz_products(1, high)
-        z_readers(1, low)
-        tz_readers(1, low)
-        z_readers(1, high)
-        tz_readers(1, high)
-        weigh(nc.vector, 1, slice(0, 2))
-        weigh(nc.vector, 1, slice(2, 4))
-        finish(nc.vector, 1, slice(0, 2))
+        w1q = quantize("w1", w1_bf)
+        dx0_codes = sb.tile([P, width(0)], U32, name="dx0_codes", align_bytes=64)
+        dx0_scales = sb.tile([P, width(0)], U8, name="dx0_scales", align_bytes=64)
+        dx0_parts = []
+        for c0, copy in ((0, nc.vector.tensor_copy), (N_MM, nc.vector.tensor_copy)):
+            part = sb.tile([P, N_MM, PACK], BF16, name="dx0_bf%d" % c0, align_bytes=64)
+            copy(
+                out=part[:].rearrange("p (c i) j -> p c j i", i=4),
+                in_=dx_raw[0][:, :, c0 : c0 + N_MM].rearrange("p j (c i) -> p c j i", i=4),
+            )
+            dx0_parts.append((c0, part))
+        product(w2_bank, 0, w2q, xq[0])
+        product(w1_bank, 0, w1q, xq[0])
+        for c0, part in dx0_parts:
+            nc.vector.quantize_mx(
+                out=dx0_codes[:, c0 : c0 + N_MM].bitcast(FP8X4),
+                scales=dx0_scales[:, c0 : c0 + N_MM],
+                in_=part[:].rearrange("p c j -> p (c j)"),
+            )
+        dxq[0] = (dx0_codes, dx0_scales)
+        low, high, every = (0, 1), (2, 3), range(G)
+        low_slice, high_slice = slice(0, 2), slice(2, 4)
+        scale_z2(0, every)
+        for pair in (low, high):
+            product(w2_bank, 1, w2q, dxq[0], pair)
+            for g in pair:
+                distance(0, (g,))
+                product(w1_bank, 1, w1q, dxq[0], (g,))
+        exponential(0, (0,))
+        round_x(1)
+        exponential(0, (1,))
+        round_dx(1)
+        cross_term(0, low)
+        inner_sum(0, low)
+        quantize_x(1)
+        weigh(nc.gpsimd, 0, low_slice)
+        product(w1_bank, 0, w1q, xq[1], low)
+        product(w2_bank, 0, w2q, xq[1], low)
+        exponential(0, high)
+        cross_term(0, high)
+        product(w1_bank, 0, w1q, xq[1], high)
+        inner_sum(0, high)
+        product(w2_bank, 0, w2q, xq[1], high)
+        weigh(nc.gpsimd, 0, high_slice)
+        finish(nc.gpsimd, 0, low_slice)
+        finish(nc.gpsimd, 0, slice(2, 3))
+        distance(1, (0,))
+        quantize_dx(1)
+        distance(1, (1, 2, 3))
+        scale_z2(1, every)
+        exponential(1, every)
+        for pair in (low, high):
+            product(w1_bank, 1, w1q, dxq[1], pair)
+            product(w2_bank, 1, w2q, dxq[1], pair)
+        for pair in (low, high):
+            cross_term(1, pair)
+            inner_sum(1, pair)
+        weigh(nc.vector, 1, low_slice)
+        weigh(nc.vector, 1, high_slice)
+        finish(nc.vector, 1, low_slice)
+        finish(nc.vector, 0, slice(3, 4))
         finish(nc.vector, 1, slice(2, 3))
         finish(nc.vector, 1, slice(3, 4))

@@ -16,10 +16,12 @@ ACT = mybir.ActivationFunctionType
 P = 128
 PACK = 4
 ROWS = D // PACK
+HALF = N // 2
 N_MM = 128
-EDGES = (0, 256, 512)
-PIECES = len(EDGES) - 1
-VECTOR_SHARE = 80
+BLOCK = 32
+FEAT = BLOCK // G
+VECTOR_SHARE = 88
+GPSIMD_SHARE = 112
 
 
 def tile_rows_tnkernrbf_kernel(tc, x, w1, w2, sh, d0, dx, og, base, out):
@@ -30,11 +32,8 @@ def tile_rows_tnkernrbf_kernel(tc, x, w1, w2, sh, d0, dx, og, base, out):
         psum = ctx.enter_context(tc.psum_pool(name="psum", bufs=1))
         ctx.enter_context(tc.manual_schedule())
 
-        def cols(k):
-            return slice(EDGES[k], EDGES[k + 1])
-
-        def width(k):
-            return EDGES[k + 1] - EDGES[k]
+        def half(array, h):
+            return array[:, :, h * HALF : (h + 1) * HALF]
 
         def load_operand(name, src):
             raw = sb.tile([P, PACK, src.shape[2]], F32, name=name + "_raw")
@@ -42,211 +41,189 @@ def tile_rows_tnkernrbf_kernel(tc, x, w1, w2, sh, d0, dx, og, base, out):
             return raw
 
         def load_rows(name, src):
-            rows = sb.tile([P, G, src.shape[2]], F32, name=name)
+            rows = sb.tile([P, G, HALF], F32, name=name)
             nc.sync.dma_start(out=rows[:], in_=src.rearrange("g m c -> m g c"))
             return rows
 
-        def interleave(copy, grouped, raw, c0, c1):
-            copy(
-                out=grouped[:, c0:c1, :].rearrange("p (c i) j -> p c j i", i=4),
-                in_=raw[:, :, c0:c1].rearrange("p j (c i) -> p c j i", i=4),
-            )
+        w2_raw = load_operand("w2", w2)
+        feat_rows = sb.tile([P, BLOCK], F32, name="feat_rows", align_bytes=64)
+        nc.gpsimd.memset(feat_rows[:], 0.0)
+        x_raw = [load_operand("x0", half(x, 0))]
+        for k, src in enumerate((sh, og)):
+            nc.sync.dma_start(out=feat_rows[k:P:FEAT, :], in_=src.rearrange("g (b i) o -> b g (i o)", i=BLOCK))
+        w1_raw = load_operand("w1", w1)
+        dx_raw = [load_operand("dx0", half(dx, 0))]
+        d0_rows = [load_rows("d0_0", half(d0, 0))]
+        x_raw.append(load_operand("x1", half(x, 1)))
+        dx_raw.append(load_operand("dx1", half(dx, 1)))
+        d0_rows.append(load_rows("d0_1", half(d0, 1)))
+        base_rows = [load_rows("base_%d" % h, half(base, h)) for h in range(2)]
 
-        def round_operand(name, raw, vector_cols):
-            n_cols = raw.shape[2]
-            grouped = sb.tile([P, n_cols, PACK], BF16, name=name + "_bf", align_bytes=64)
-            if vector_cols < n_cols:
-                interleave(nc.scalar.copy, grouped, raw, vector_cols, n_cols)
-            if vector_cols > 0:
-                interleave(nc.vector.tensor_copy, grouped, raw, 0, vector_cols)
+        def work(name):
+            return [sb.tile([P, G, HALF], F32, name=name + str(h)) for h in range(2)]
+
+        negq = work("negq")
+        gauss = work("gauss")
+        z2s = work("z2s")
+        cross = work("cross")
+        inner = work("inner")
+        change = work("change")
+        res = work("res")
+        feat = sb.tile([P, G, FEAT], F32, name="feat", align_bytes=64)
+        coef = sb.tile([P, G], F32, name="coef")
+        w1_bank = [psum.tile([P, 2, HALF], F32, name="w1_bank%d" % g) for g in range(G)]
+        w2_bank = [psum.tile([P, 2, HALF], F32, name="w2_bank%d" % g) for g in range(G)]
+        of_x, of_dx = 0, 1
+
+        def gpsimd_copy(out, in_):
+            nc.gpsimd.tensor_scalar(out=out, in0=in_, scalar1=1.0, scalar2=0.0, op0=ALU.mult, op1=ALU.add)
+
+        def round_columns(name, raw, shares):
+            grouped = sb.tile([P, raw.shape[2], PACK], BF16, name=name + "_bf", align_bytes=64)
+            for copy, c0, c1 in shares:
+                copy(out=grouped[:, c0:c1, :], in_=raw[:, :, c0:c1].rearrange("p j c -> p c j"))
             return grouped
 
-        def quantize(name, grouped):
-            n_cols = grouped.shape[1]
+        def round_on_vector_and_scalar(name, raw):
+            n_cols = raw.shape[2]
+            cut = VECTOR_SHARE * n_cols // 128
+            return round_columns(name, raw, [(nc.scalar.copy, cut, n_cols), (nc.vector.tensor_copy, 0, cut)])
+
+        def mx_operand(name, n_cols):
             codes = sb.tile([P, n_cols], U32, name=name + "_codes", align_bytes=64)
             scales = sb.tile([P, n_cols], U8, name=name + "_scales", align_bytes=64)
-            nc.vector.quantize_mx(
-                out=codes[:].bitcast(FP8X4), scales=scales[:], in_=grouped[:].rearrange("p c j -> p (c j)")
-            )
             return codes, scales
 
-        def product(banks, which, w, v, groups=range(G)):
-            for c0 in range(0, v[0].shape[1], N_MM):
-                span = slice(c0, c0 + N_MM)
+        def quantize_into(operand, c0, grouped):
+            codes, scales = operand
+            cols = slice(c0, c0 + grouped.shape[1])
+            nc.vector.quantize_mx(
+                out=codes[:, cols].bitcast(FP8X4),
+                scales=scales[:, cols],
+                in_=grouped[:].rearrange("p c j -> p (c j)"),
+            )
+
+        def quantize(name, grouped):
+            operand = mx_operand(name, grouped.shape[1])
+            quantize_into(operand, 0, grouped)
+            return operand
+
+        def product(banks, place, weights, moving, groups):
+            for c0 in range(0, HALF, N_MM):
+                cols = slice(c0, c0 + N_MM)
                 for g in groups:
                     rows = slice(ROWS * g, ROWS * (g + 1))
                     nc.tensor.matmul_mx(
-                        out=banks[g][:, which, span],
-                        lhsT=w[0][rows, :].bitcast(FP8X4),
-                        lhsT_scale=w[1][rows, :],
-                        rhs=v[0][rows, span].bitcast(FP8X4),
-                        rhs_scale=v[1][rows, span],
+                        out=banks[g][:, place, cols],
+                        lhsT=weights[0][rows, :].bitcast(FP8X4),
+                        lhsT_scale=weights[1][rows, :],
+                        rhs=moving[0][rows, cols].bitcast(FP8X4),
+                        rhs_scale=moving[1][rows, cols],
                         start=True,
                         stop=True,
                     )
 
-        x_raw, dx_raw, d0_sb, base_sb = {}, {}, {}, {}
-
-        def load_x(k):
-            x_raw[k] = load_operand("x%d" % k, x[:, :, cols(k)])
-
-        def load_dx(k):
-            dx_raw[k] = load_operand("dx%d" % k, dx[:, :, cols(k)])
-
-        def load_d0(k0, k1):
-            rows = load_rows("d0_%d" % k0, d0[:, :, EDGES[k0] : EDGES[k1]])
-            for k in range(k0, k1):
-                d0_sb[k] = rows[:, :, EDGES[k] - EDGES[k0] : EDGES[k + 1] - EDGES[k0]]
-
-        def load_base(k0, k1):
-            rows = load_rows("base_%d" % k0, base[:, :, EDGES[k0] : EDGES[k1]])
-            for k in range(k0, k1):
-                base_sb[k] = rows[:, :, EDGES[k] - EDGES[k0] : EDGES[k + 1] - EDGES[k0]]
-
-        w2_raw = load_operand("w2", w2)
-        feat_rows = sb.tile([P, 32], F32, name="feat_rows", align_bytes=64)
-        nc.gpsimd.memset(feat_rows[:], 0.0)
-        load_x(0)
-        for k, src in enumerate((sh, og)):
-            nc.sync.dma_start(out=feat_rows[k:P:8, :], in_=src.rearrange("g (b i) o -> b g (i o)", i=32))
-        w1_raw = load_operand("w1", w1)
-        load_dx(0)
-        load_d0(0, 1)
-        load_x(1)
-        load_dx(1)
-        load_d0(1, 2)
-        load_base(0, 1)
-        load_base(1, 2)
-
-        def work(name):
-            return [sb.tile([P, G, width(k)], F32, name=name + str(k)) for k in range(PIECES)]
-
-        negq, gauss, z2s, cross, inner, xh, res = [
-            work(s) for s in ("negq", "gauss", "z2s", "cross", "inner", "xh", "res")
-        ]
-        feat = sb.tile([P, G, 8], F32, name="feat", align_bytes=64)
-        coef = sb.tile([P, G, 8], F32, name="coef")
-        w1_bank = [psum.tile([P, 2, 256], F32, name="w1_bank%d" % g) for g in range(G)]
-        w2_bank = [psum.tile([P, 2, 256], F32, name="w2_bank%d" % g) for g in range(G)]
-        xq, dxq, x_bf, dx_bf = {}, {}, {}, {}
-
-        def distance(k, groups):
+        def distance(h, groups):
             for g in groups:
                 nc.vector.scalar_tensor_tensor(
-                    out=negq[k][:, g, :], in0=w1_bank[g][:, 0, : width(k)], scalar=2.0, in1=d0_sb[k][:, g, :],
+                    out=negq[h][:, g, :], in0=w1_bank[g][:, of_x, :], scalar=2.0, in1=d0_rows[h][:, g, :],
                     op0=ALU.mult, op1=ALU.subtract,
                 )
 
-        def exponential(k, groups):
+        def exponential(h, groups):
             for g in groups:
-                nc.scalar.activation(out=gauss[k][:, g, :], in_=negq[k][:, g, :], func=ACT.Exp, scale=feat[:, g, 0:1])
+                nc.scalar.activation(out=gauss[h][:, g, :], in_=negq[h][:, g, :], func=ACT.Exp, scale=feat[:, g, 0:1])
 
-        def scale_z2(k, groups):
+        def scale_z2(h, groups):
             for g in groups:
                 nc.scalar.activation(
-                    out=z2s[k][:, g, :], in_=w2_bank[g][:, 0, : width(k)], func=ACT.Copy, scale=coef[:, g, 0:1]
+                    out=z2s[h][:, g, :], in_=w2_bank[g][:, of_x, :], func=ACT.Copy, scale=coef[:, g : g + 1]
                 )
 
-        def cross_term(k, groups):
+        def cross_term(h, groups):
             for g in groups:
                 nc.vector.tensor_tensor(
-                    out=cross[k][:, g, :], in0=w1_bank[g][:, 1, : width(k)], in1=z2s[k][:, g, :], op=ALU.mult
+                    out=cross[h][:, g, :], in0=w1_bank[g][:, of_dx, :], in1=z2s[h][:, g, :], op=ALU.mult
                 )
 
-        def inner_sum(k, groups):
+        def inner_sum(h, groups):
             for g in groups:
                 nc.vector.scalar_tensor_tensor(
-                    out=inner[k][:, g, :], in0=w2_bank[g][:, 1, : width(k)], scalar=feat[:, g, 1:2],
-                    in1=cross[k][:, g, :], op0=ALU.mult, op1=ALU.add,
+                    out=inner[h][:, g, :], in0=w2_bank[g][:, of_dx, :], scalar=feat[:, g, 1:2],
+                    in1=cross[h][:, g, :], op0=ALU.mult, op1=ALU.add,
                 )
 
-        def weigh(engine, k, gs=slice(0, G)):
-            engine.tensor_tensor(out=xh[k][:, gs, :], in0=inner[k][:, gs, :], in1=gauss[k][:, gs, :], op=ALU.mult)
+        def weigh(engine, h, groups):
+            gs = slice(groups[0], groups[-1] + 1)
+            engine.tensor_tensor(out=change[h][:, gs, :], in0=inner[h][:, gs, :], in1=gauss[h][:, gs, :], op=ALU.mult)
 
-        def finish(engine, k, gs=slice(0, G)):
-            engine.tensor_tensor(out=res[k][:, gs, :], in0=xh[k][:, gs, :], in1=base_sb[k][:, gs, :], op=ALU.add)
-            nc.sync.dma_start(out=out[gs, :, cols(k)].rearrange("g m c -> m g c"), in_=res[k][:, gs, :])
+        def finish(engine, h, groups):
+            gs = slice(groups[0], groups[-1] + 1)
+            engine.tensor_tensor(out=res[h][:, gs, :], in0=change[h][:, gs, :], in1=base_rows[h][:, gs, :], op=ALU.add)
+            nc.sync.dma_start(out=half(out, h)[gs].rearrange("g m c -> m g c"), in_=res[h][:, gs, :])
 
-        def round_x(k, vector_cols=0):
-            x_bf[k] = round_operand("x%d" % k, x_raw[k], vector_cols)
+        low, high, every = (0, 1), (2, 3), (0, 1, 2, 3)
 
-        def round_dx(k, vector_cols=0):
-            dx_bf[k] = round_operand("dx%d" % k, dx_raw[k], vector_cols)
-
-        def quantize_x(k):
-            xq[k] = quantize("x%d" % k, x_bf[k])
-
-        def quantize_dx(k):
-            dxq[k] = quantize("dx%d" % k, dx_bf[k])
-
-        w2q = quantize("w2", round_operand("w2", w2_raw, VECTOR_SHARE))
-        round_x(0, VECTOR_SHARE * width(0) // 128)
-        quantize_x(0)
+        w2q = quantize("w2", round_on_vector_and_scalar("w2", w2_raw))
+        x0q = quantize("x0", round_on_vector_and_scalar("x0", x_raw[0]))
         nc.vector.transpose(feat[:].rearrange("p g k -> p (g k)"), feat_rows[:])
-        w1_bf = round_operand("w1", w1_raw, VECTOR_SHARE)
+        w1_bf = round_on_vector_and_scalar("w1", w1_raw)
         nc.vector.scalar_tensor_tensor(
-            out=coef[:, :, 0], in0=feat[:, :, 0], scalar=2.0, in1=feat[:, :, 1], op0=ALU.mult, op1=ALU.mult
+            out=coef[:], in0=feat[:, :, 0], scalar=2.0, in1=feat[:, :, 1], op0=ALU.mult, op1=ALU.mult
         )
         w1q = quantize("w1", w1_bf)
-        dx0_codes = sb.tile([P, width(0)], U32, name="dx0_codes", align_bytes=64)
-        dx0_scales = sb.tile([P, width(0)], U8, name="dx0_scales", align_bytes=64)
-        dx0_parts = []
-        for c0, copy in ((0, nc.vector.tensor_copy), (N_MM, nc.vector.tensor_copy)):
-            part = sb.tile([P, N_MM, PACK], BF16, name="dx0_bf%d" % c0, align_bytes=64)
-            copy(
-                out=part[:].rearrange("p (c i) j -> p c j i", i=4),
-                in_=dx_raw[0][:, :, c0 : c0 + N_MM].rearrange("p j (c i) -> p c j i", i=4),
-            )
-            dx0_parts.append((c0, part))
-        product(w2_bank, 0, w2q, xq[0])
-        product(w1_bank, 0, w1q, xq[0])
-        for c0, part in dx0_parts:
-            nc.vector.quantize_mx(
-                out=dx0_codes[:, c0 : c0 + N_MM].bitcast(FP8X4),
-                scales=dx0_scales[:, c0 : c0 + N_MM],
-                in_=part[:].rearrange("p c j -> p (c j)"),
-            )
-        dxq[0] = (dx0_codes, dx0_scales)
-        low, high, every = (0, 1), (2, 3), range(G)
-        low_slice, high_slice = slice(0, 2), slice(2, 4)
+        product(w2_bank, of_x, w2q, x0q, every)
+        product(w1_bank, of_x, w1q, x0q, every)
+        dx0q = mx_operand("dx0", HALF)
+        dx0_parts = [
+            round_columns("dx0_%d" % c0, dx_raw[0][:, :, c0 : c0 + N_MM], [(nc.vector.tensor_copy, 0, N_MM)])
+            for c0 in range(0, HALF, N_MM)
+        ]
+        for i, part in enumerate(dx0_parts):
+            quantize_into(dx0q, i * N_MM, part)
+
         scale_z2(0, every)
         for pair in (low, high):
-            product(w2_bank, 1, w2q, dxq[0], pair)
+            product(w2_bank, of_dx, w2q, dx0q, pair)
             for g in pair:
                 distance(0, (g,))
-                product(w1_bank, 1, w1q, dxq[0], (g,))
+                product(w1_bank, of_dx, w1q, dx0q, (g,))
+
         exponential(0, (0,))
-        round_x(1)
+        x1_bf = round_columns("x1", x_raw[1], [(nc.scalar.copy, GPSIMD_SHARE, HALF), (gpsimd_copy, 0, GPSIMD_SHARE)])
         exponential(0, (1,))
-        round_dx(1)
+        dx1_bf = round_columns("dx1", dx_raw[1], [(nc.scalar.copy, 0, HALF)])
         cross_term(0, low)
         inner_sum(0, low)
-        quantize_x(1)
-        weigh(nc.gpsimd, 0, low_slice)
-        product(w1_bank, 0, w1q, xq[1], low)
-        product(w2_bank, 0, w2q, xq[1], low)
+        x1q = quantize("x1", x1_bf)
+        weigh(nc.gpsimd, 0, low)
+        product(w1_bank, of_x, w1q, x1q, low)
+        product(w2_bank, of_x, w2q, x1q, low)
         exponential(0, high)
         cross_term(0, high)
-        product(w1_bank, 0, w1q, xq[1], high)
+        product(w1_bank, of_x, w1q, x1q, high)
         inner_sum(0, high)
-        product(w2_bank, 0, w2q, xq[1], high)
-        weigh(nc.gpsimd, 0, high_slice)
-        finish(nc.gpsimd, 0, low_slice)
-        finish(nc.gpsimd, 0, slice(2, 3))
+        product(w2_bank, of_x, w2q, x1q, high)
+        weigh(nc.gpsimd, 0, high)
+        finish(nc.gpsimd, 0, low)
+        finish(nc.gpsimd, 0, (2,))
+
         distance(1, (0,))
-        quantize_dx(1)
+        dx1q = quantize("dx1", dx1_bf)
         distance(1, (1, 2, 3))
         scale_z2(1, every)
         exponential(1, every)
         for pair in (low, high):
-            product(w1_bank, 1, w1q, dxq[1], pair)
-            product(w2_bank, 1, w2q, dxq[1], pair)
+            product(w1_bank, of_dx, w1q, dx1q, pair)
+            product(w2_bank, of_dx, w2q, dx1q, pair)
         for pair in (low, high):
             cross_term(1, pair)
             inner_sum(1, pair)
-        weigh(nc.vector, 1, low_slice)
-        weigh(nc.vector, 1, high_slice)
-        finish(nc.vector, 1, low_slice)
-        finish(nc.vector, 0, slice(3, 4))
-        finish(nc.vector, 1, slice(2, 3))
-        finish(nc.vector, 1, slice(3, 4))
+
+        finish(nc.vector, 0, (3,))
+        weigh(nc.vector, 1, low)
+        weigh(nc.vector, 1, (2,))
+        finish(nc.vector, 1, low)
+        weigh(nc.vector, 1, (3,))
+        finish(nc.vector, 1, (2,))
+        finish(nc.vector, 1, (3,))

@@ -18,6 +18,7 @@ PACK = 4
 ROWS = D // PACK
 HALF = N // 2
 N_MM = 128
+RUN = 4
 BLOCK = 32
 FEAT = BLOCK // G
 VECTOR_SHARE = 88
@@ -81,7 +82,10 @@ def tile_rows_tnkernrbf_kernel(tc, x, w1, w2, sh, d0, dx, og, base, out):
         def round_columns(name, raw, shares):
             grouped = sb.tile([P, raw.shape[2], PACK], BF16, name=name + "_bf", align_bytes=64)
             for copy, c0, c1 in shares:
-                copy(out=grouped[:, c0:c1, :], in_=raw[:, :, c0:c1].rearrange("p j c -> p c j"))
+                copy(
+                    out=grouped[:, c0:c1, :].rearrange("p (c i) j -> p c j i", i=RUN),
+                    in_=raw[:, :, c0:c1].rearrange("p j (c i) -> p c j i", i=RUN),
+                )
             return grouped
 
         def round_on_vector_and_scalar(name, raw):

from contextlib import ExitStack

import concourse.mybir as mybir

G, D, M, N = 4, 128, 128, 512
FLOPS = 4 * 2 * G * D * M * N

F32 = mybir.dt.float32
BF16 = mybir.dt.bfloat16
U32 = mybir.dt.uint32
U8 = mybir.dt.uint8
FP8X4 = mybir.dt.float8_e4m3fn_x4
ALU = mybir.AluOpType
ACT = mybir.ActivationFunctionType

P = 128
PACK = 4
ROWS = D // PACK
HALF = N // 2
N_MM = 128
RUN = 4
BLOCK = 32
FEAT = BLOCK // G
VECTOR_SHARE = 88
GPSIMD_SHARE = 112


def tile_rows_tnkernrbf_kernel(tc, x, w1, w2, sh, d0, dx, og, base, out):
    nc = tc.nc

    with ExitStack() as ctx:
        sb = ctx.enter_context(tc.tile_pool(name="sb", bufs=1))
        psum = ctx.enter_context(tc.psum_pool(name="psum", bufs=1))
        ctx.enter_context(tc.manual_schedule())

        def half(array, h):
            return array[:, :, h * HALF : (h + 1) * HALF]

        def load_operand(name, src):
            raw = sb.tile([P, PACK, src.shape[2]], F32, name=name + "_raw")
            nc.sync.dma_start(out=raw[:], in_=src.rearrange("g (p j) c -> (g p) j c", j=PACK))
            return raw

        def load_rows(name, src):
            rows = sb.tile([P, G, HALF], F32, name=name)
            nc.sync.dma_start(out=rows[:], in_=src.rearrange("g m c -> m g c"))
            return rows

        w2_raw = load_operand("w2", w2)
        feat_rows = sb.tile([P, BLOCK], F32, name="feat_rows", align_bytes=64)
        nc.gpsimd.memset(feat_rows[:], 0.0)
        x_raw = [load_operand("x0", half(x, 0))]
        for k, src in enumerate((sh, og)):
            nc.sync.dma_start(out=feat_rows[k:P:FEAT, :], in_=src.rearrange("g (b i) o -> b g (i o)", i=BLOCK))
        w1_raw = load_operand("w1", w1)
        dx_raw = [load_operand("dx0", half(dx, 0))]
        d0_rows = [load_rows("d0_0", half(d0, 0))]
        x_raw.append(load_operand("x1", half(x, 1)))
        dx_raw.append(load_operand("dx1", half(dx, 1)))
        d0_rows.append(load_rows("d0_1", half(d0, 1)))
        base_rows = [load_rows("base_%d" % h, half(base, h)) for h in range(2)]

        def work(name):
            return [sb.tile([P, G, HALF], F32, name=name + str(h)) for h in range(2)]

        negq = work("negq")
        gauss = work("gauss")
        z2s = work("z2s")
        cross = work("cross")
        inner = work("inner")
        change = work("change")
        res = work("res")
        feat = sb.tile([P, G, FEAT], F32, name="feat", align_bytes=64)
        coef = sb.tile([P, G], F32, name="coef")
        w1_bank = [psum.tile([P, 2, HALF], F32, name="w1_bank%d" % g) for g in range(G)]
        w2_bank = [psum.tile([P, 2, HALF], F32, name="w2_bank%d" % g) for g in range(G)]
        of_x, of_dx = 0, 1

        def gpsimd_copy(out, in_):
            nc.gpsimd.tensor_scalar(out=out, in0=in_, scalar1=1.0, scalar2=0.0, op0=ALU.mult, op1=ALU.add)

        def round_columns(name, raw, shares):
            grouped = sb.tile([P, raw.shape[2], PACK], BF16, name=name + "_bf", align_bytes=64)
            for copy, c0, c1 in shares:
                copy(
                    out=grouped[:, c0:c1, :].rearrange("p (c i) j -> p c j i", i=RUN),
                    in_=raw[:, :, c0:c1].rearrange("p j (c i) -> p c j i", i=RUN),
                )
            return grouped

        def round_on_vector_and_scalar(name, raw):
            n_cols = raw.shape[2]
            cut = VECTOR_SHARE * n_cols // 128
            return round_columns(name, raw, [(nc.scalar.copy, cut, n_cols), (nc.vector.tensor_copy, 0, cut)])

        def mx_operand(name, n_cols):
            codes = sb.tile([P, n_cols], U32, name=name + "_codes", align_bytes=64)
            scales = sb.tile([P, n_cols], U8, name=name + "_scales", align_bytes=64)
            return codes, scales

        def quantize_into(operand, c0, grouped):
            codes, scales = operand
            cols = slice(c0, c0 + grouped.shape[1])
            nc.vector.quantize_mx(
                out=codes[:, cols].bitcast(FP8X4),
                scales=scales[:, cols],
                in_=grouped[:].rearrange("p c j -> p (c j)"),
            )

        def quantize(name, grouped):
            operand = mx_operand(name, grouped.shape[1])
            quantize_into(operand, 0, grouped)
            return operand

        def product(banks, place, weights, moving, groups):
            for c0 in range(0, HALF, N_MM):
                cols = slice(c0, c0 + N_MM)
                for g in groups:
                    rows = slice(ROWS * g, ROWS * (g + 1))
                    nc.tensor.matmul_mx(
                        out=banks[g][:, place, cols],
                        lhsT=weights[0][rows, :].bitcast(FP8X4),
                        lhsT_scale=weights[1][rows, :],
                        rhs=moving[0][rows, cols].bitcast(FP8X4),
                        rhs_scale=moving[1][rows, cols],
                        start=True,
                        stop=True,
                    )

        def distance(h, groups):
            for g in groups:
                nc.vector.scalar_tensor_tensor(
                    out=negq[h][:, g, :], in0=w1_bank[g][:, of_x, :], scalar=2.0, in1=d0_rows[h][:, g, :],
                    op0=ALU.mult, op1=ALU.subtract,
                )

        def exponential(h, groups):
            for g in groups:
                nc.scalar.activation(out=gauss[h][:, g, :], in_=negq[h][:, g, :], func=ACT.Exp, scale=feat[:, g, 0:1])

        def scale_z2(h, groups):
            for g in groups:
                nc.scalar.activation(
                    out=z2s[h][:, g, :], in_=w2_bank[g][:, of_x, :], func=ACT.Copy, scale=coef[:, g : g + 1]
                )

        def cross_term(h, groups):
            for g in groups:
                nc.vector.tensor_tensor(
                    out=cross[h][:, g, :], in0=w1_bank[g][:, of_dx, :], in1=z2s[h][:, g, :], op=ALU.mult
                )

        def inner_sum(h, groups):
            for g in groups:
                nc.vector.scalar_tensor_tensor(
                    out=inner[h][:, g, :], in0=w2_bank[g][:, of_dx, :], scalar=feat[:, g, 1:2],
                    in1=cross[h][:, g, :], op0=ALU.mult, op1=ALU.add,
                )

        def weigh(engine, h, groups):
            gs = slice(groups[0], groups[-1] + 1)
            engine.tensor_tensor(out=change[h][:, gs, :], in0=inner[h][:, gs, :], in1=gauss[h][:, gs, :], op=ALU.mult)

        def finish(engine, h, groups):
            gs = slice(groups[0], groups[-1] + 1)
            engine.tensor_tensor(out=res[h][:, gs, :], in0=change[h][:, gs, :], in1=base_rows[h][:, gs, :], op=ALU.add)
            nc.sync.dma_start(out=half(out, h)[gs].rearrange("g m c -> m g c"), in_=res[h][:, gs, :])

        low, high, every = (0, 1), (2, 3), (0, 1, 2, 3)

        w2q = quantize("w2", round_on_vector_and_scalar("w2", w2_raw))
        x0q = quantize("x0", round_on_vector_and_scalar("x0", x_raw[0]))
        nc.vector.transpose(feat[:].rearrange("p g k -> p (g k)"), feat_rows[:])
        w1_bf = round_on_vector_and_scalar("w1", w1_raw)
        nc.vector.scalar_tensor_tensor(
            out=coef[:], in0=feat[:, :, 0], scalar=2.0, in1=feat[:, :, 1], op0=ALU.mult, op1=ALU.mult
        )
        w1q = quantize("w1", w1_bf)
        product(w2_bank, of_x, w2q, x0q, every)
        product(w1_bank, of_x, w1q, x0q, every)
        dx0q = mx_operand("dx0", HALF)
        dx0_parts = [
            round_columns("dx0_%d" % c0, dx_raw[0][:, :, c0 : c0 + N_MM], [(nc.vector.tensor_copy, 0, N_MM)])
            for c0 in range(0, HALF, N_MM)
        ]
        for i, part in enumerate(dx0_parts):
            quantize_into(dx0q, i * N_MM, part)

        scale_z2(0, every)
        for pair in (low, high):
            product(w2_bank, of_dx, w2q, dx0q, pair)
            for g in pair:
                distance(0, (g,))
                product(w1_bank, of_dx, w1q, dx0q, (g,))

        exponential(0, (0,))
        x1_bf = round_columns("x1", x_raw[1], [(nc.scalar.copy, GPSIMD_SHARE, HALF), (gpsimd_copy, 0, GPSIMD_SHARE)])
        exponential(0, (1,))
        dx1_bf = round_columns("dx1", dx_raw[1], [(nc.scalar.copy, 0, HALF)])
        cross_term(0, low)
        inner_sum(0, low)
        x1q = quantize("x1", x1_bf)
        weigh(nc.gpsimd, 0, low)
        product(w1_bank, of_x, w1q, x1q, low)
        product(w2_bank, of_x, w2q, x1q, low)
        exponential(0, high)
        cross_term(0, high)
        product(w1_bank, of_x, w1q, x1q, high)
        inner_sum(0, high)
        product(w2_bank, of_x, w2q, x1q, high)
        weigh(nc.gpsimd, 0, high)
        finish(nc.gpsimd, 0, low)
        finish(nc.gpsimd, 0, (2,))

        distance(1, (0,))
        dx1q = quantize("dx1", dx1_bf)
        distance(1, (1, 2, 3))
        scale_z2(1, every)
        exponential(1, every)
        for pair in (low, high):
            product(w1_bank, of_dx, w1q, dx1q, pair)
            product(w2_bank, of_dx, w2q, dx1q, pair)
        for pair in (low, high):
            cross_term(1, pair)
            inner_sum(1, pair)

        finish(nc.vector, 0, (3,))
        weigh(nc.vector, 1, low)
        weigh(nc.vector, 1, (2,))
        finish(nc.vector, 1, low)
        weigh(nc.vector, 1, (3,))
        finish(nc.vector, 1, (2,))
        finish(nc.vector, 1, (3,))
